import numpy as np
import ml_dtypes


def mxq(x, axis, fmt="e4m3"):
    dtype, down = {"e4m3": (ml_dtypes.float8_e4m3fn, 7), "e5m2": (ml_dtypes.float8_e5m2, 14)}[fmt]
    v = np.moveaxis(np.asarray(x, np.float32).astype(ml_dtypes.bfloat16).astype(np.float64), axis, -1)
    blocks = v.reshape(v.shape[:-1] + (-1, 32))
    amax = np.abs(blocks).max(-1, keepdims=True)
    byte = np.maximum(np.where(amax > 0, np.frexp(amax)[1] - 1 + 127, 0) - down, 1)
    scale = np.exp2(byte - 127.0)
    codes = (blocks / scale).astype(np.float32).astype(dtype).astype(np.float64)
    return np.moveaxis((codes * scale).reshape(v.shape), -1, axis)


WIDE = False


def mx_kscale(k, group=512):
    if not WIDE:
        return np.ones(k)
    levels = np.array([10, -10, 5, -5, 0])
    if group != 512:
        return np.exp2(np.random.permutation(np.resize(levels, k // group))).repeat(group)
    if k % 512:
        return np.exp2(np.random.permutation(np.resize(levels, k // 32))).repeat(32)
    a = np.empty((k // 512, 16))
    for p in range(k // 512):
        a[p, :8] = np.random.permutation(np.resize(levels, 8))
        for g in range(8):
            far = levels[np.abs(levels - a[p, g]) >= 10]
            a[p, g + 8] = far[np.random.randint(len(far))]
    return np.exp2(a.ravel()).repeat(32)


def f64(x):
    return np.asarray(x).astype(np.float64)


def striped(idx):
    return np.tile(np.asarray(idx).reshape(-1, 16).T, (8, 1)).astype(np.uint16)


def unstriped(offs):
    return offs[:16].T.reshape(-1).astype(np.int64)


H, KV, D, NQ, N = 2, 2, 256, 512, 512


def setup_inputs():
    n = np.random.standard_normal
    s = mx_kscale(D, 0)[:, None]
    u = mx_kscale(N)
    t = np.random.uniform(0.5, 2.0, N) * u
    v = n((KV, N, 128))
    return {
        "qT": (n((H, D, NQ)) * s * (0.70 / np.sqrt(D))).astype(np.float32),
        "kT": (n((KV, D, N)) / s).astype(np.float32),
        "t": t.reshape(N, 1).astype(np.float32),
        "v": (v / t[:, None]).astype(np.float32),
        "gn": np.tile(np.random.uniform(0.5, 2.0, 128), (128, 1)).astype(np.float32),
    }


def reference(qT, kT, t, v, gn):
    a = mxq(f64(kT), 1, "e4m3").transpose(0, 2, 1) @ mxq(f64(qT), 1, "e4m3")
    p = a / (1.0 + np.exp(-a))
    w = p * f64(t)
    y = mxq(w, 1, "e4m3").transpose(0, 2, 1) @ mxq(f64(v), 1, "e4m3")
    y = y / 16.0
    y = y / np.sqrt(np.mean(np.square(y), -1, keepdims=True) + 1e-5) * f64(gn)[:1]
    return y

@@ -1,0 +1,255 @@
+from contextlib import ExitStack
+
+import concourse.mybir as mybir
+
+H, D, NQ, NT, E = 2, 256, 512, 512, 128
+FLOPS = 2 * H * NQ * NT * (D + E)
+
+F32 = mybir.dt.float32
+BF16 = mybir.dt.bfloat16
+U32 = mybir.dt.uint32
+U8 = mybir.dt.uint8
+FP8X4 = mybir.dt.float8_e4m3fn_x4
+ACT = mybir.ActivationFunctionType
+ALU = mybir.AluOpType
+
+P = 128
+PACK = 4
+ROWS = D // PACK
+QT = 128
+TILES = NQ // QT
+UNITS = TILES * H
+HALF = NT // 2
+SLOTS = HALF // PACK
+EPS = 1e-5 * 16.0 * 16.0
+K_PIECES = [(0, 256), (256, 384), (384, 512)]
+
+
+def tile_rows_a_silu_onorm_kernel(tc, qT, kT, t, v, gn, out):
+    nc = tc.nc
+    with ExitStack() as ctx:
+        sb = ctx.enter_context(tc.tile_pool(name="sb", bufs=1))
+        ps = ctx.enter_context(tc.psum_pool(name="ps", bufs=1))
+        ctx.enter_context(tc.manual_schedule())
+
+        def tiles(name, n, shape, dtype):
+            return [sb.tile(shape, dtype, name="%s%d" % (name, i), align_bytes=64) for i in range(n)]
+
+        k_raw = [
+            sb.tile([P, PACK, n1 - n0], F32, name="k_raw%d" % i, align_bytes=64)
+            for i, (n0, n1) in enumerate(K_PIECES)
+        ]
+        q_raw = tiles("q_raw", TILES, [P, PACK, QT], F32)
+        v_raw = tiles("v_raw", H, [P, PACK, E], F32)
+        t_sb = sb.tile([P, 1, PACK], F32, name="t_sb")
+        gn_sb = sb.tile([P, E], F32, name="gn_sb")
+        k_bf = tiles("k_bf", 2, [P, PACK, SLOTS, PACK], BF16)
+        q_bf = tiles("q_bf", TILES, [P, QT, PACK], BF16)
+        v_bf = tiles("v_bf", H, [P, E, PACK], BF16)
+        k_codes = tiles("k_codes", PACK, [P, P], U32)
+        k_scales = tiles("k_scales", PACK, [P, P], U8)
+        q_codes = tiles("q_codes", TILES, [P, QT], U32)
+        q_scales = tiles("q_scales", TILES, [P, QT], U8)
+        v_codes = tiles("v_codes", H, [P, E], U32)
+        v_scales = tiles("v_scales", H, [P, E], U8)
+        p_sb = tiles("p_sb", UNITS, [P, QT, PACK], F32)
+        w_bf = tiles("w_bf", UNITS, [P, QT, PACK], BF16)
+        w_codes = tiles("w_codes", UNITS, [P, QT], U32)
+        w_scales = tiles("w_scales", UNITS, [P, QT], U8)
+        squares = tiles("squares", UNITS, [P, E], BF16)
+        sums = sb.tile([P, UNITS], F32, name="sums")
+        rstd = sb.tile([P, UNITS], F32, name="rstd")
+        zero_in = sb.tile([P, 1], F32, name="zero_in")
+        zero = sb.tile([P, 1], F32, name="zero")
+        o_sb = tiles("o_sb", TILES, [P, H, E], F32)
+        score_banks = [
+            [ps.tile([P, PACK, QT], F32, name="score%d_%d" % (h, i)) for i in range(2)] for h in range(H)
+        ]
+        y_banks = [ps.tile([P, H, E], F32, name="y%d" % c) for c in range(TILES)]
+
+        k_hbm = kT.rearrange("h (p j) n -> (h p) j n", j=PACK)
+        q_hbm = qT.rearrange("h (p j) n -> (h p) j n", j=PACK)
+
+        def load_k(a):
+            n0, n1 = K_PIECES[a]
+            nc.sync.dma_start(out=k_raw[a][:], in_=k_hbm[:, :, n0:n1])
+
+        def load_q(c):
+            nc.sync.dma_start(out=q_raw[c][:], in_=q_hbm[:, :, c * QT : (c + 1) * QT])
+
+        def load_v(h):
+            nc.sync.dma_start(out=v_raw[h][:], in_=v[h].rearrange("(p j) e -> p j e", j=PACK))
+
+        def copier(engine):
+            return nc.vector.tensor_copy if engine == "vector" else nc.scalar.copy
+
+        def cast_k(a):
+            n0, n1 = K_PIECES[a]
+            half, s0 = divmod(n0 // PACK, SLOTS)
+            nc.vector.tensor_copy(
+                out=k_bf[half][:, :, s0 : s0 + (n1 - n0) // PACK, :].rearrange("p r s j -> p s j r"),
+                in_=k_raw[a][:].rearrange("p j (s r) -> p s j r", r=PACK),
+            )
+
+        def cast(engine, raw, bf, c0, c1):
+            copier(engine)(
+                out=bf[:, c0:c1, :].rearrange("p (g i) j -> p g j i", i=4),
+                in_=raw[:, :, c0:c1].rearrange("p j (g i) -> p g j i", i=4),
+            )
+
+        def quantize(codes, scales, bf):
+            nc.vector.quantize_mx(out=codes.bitcast(FP8X4), scales=scales, in_=bf.rearrange("p c j -> p (c j)"))
+
+        def quantize_k(a):
+            cols = slice(a * SLOTS, (a + 1) * SLOTS)
+            for r in range(PACK):
+                quantize(k_codes[r][:, cols], k_scales[r][:, cols], k_bf[a][:, r, :, :])
+
+        def quantize_q(c):
+            quantize(q_codes[c][:], q_scales[c][:], q_bf[c][:])
+
+        def quantize_v(h):
+            quantize(v_codes[h][:], v_scales[h][:], v_bf[h][:])
+
+        def scores(c):
+            for h in range(H):
+                for r in range(PACK):
+                    rows = slice(ROWS * h, ROWS * (h + 1))
+                    nc.tensor.matmul_mx(
+                        out=score_banks[h][c % 2][:, r, :],
+                        lhsT=k_codes[r][rows, :].bitcast(FP8X4),
+                        lhsT_scale=k_scales[r][rows, :],
+                        rhs=q_codes[c][rows, :].bitcast(FP8X4),
+                        rhs_scale=q_scales[c][rows, :],
+                        start=True,
+                        stop=True,
+                    )
+
+        def silu(u):
+            c, h = divmod(u, H)
+            nc.scalar.activation(
+                out=p_sb[u][:], in_=score_banks[h][c % 2][:].rearrange("p r q -> p q r"), func=ACT.Silu
+            )
+
+        def weigh(u):
+            nc.vector.tensor_tensor(
+                out=w_bf[u][:], in0=p_sb[u][:], in1=t_sb[:].to_broadcast([P, QT, PACK]), op=ALU.mult
+            )
+
+        def product(u):
+            c, h = divmod(u, H)
+            quantize(w_codes[u][:], w_scales[u][:], w_bf[u][:])
+            nc.tensor.matmul_mx(
+                out=y_banks[c][:, h, :],
+                lhsT=w_codes[u][:].bitcast(FP8X4),
+                lhsT_scale=w_scales[u][:],
+                rhs=v_codes[h][:].bitcast(FP8X4),
+                rhs_scale=v_scales[h][:],
+                start=True,
+                stop=True,
+            )
+
+        def square(u):
+            c, h = divmod(u, H)
+            nc.scalar.activation(
+                out=squares[u][:], in_=y_banks[c][:, h, :], func=ACT.Square, bias=zero[:], accum_out=sums[:, u : u + 1]
+            )
+
+        def inverse_root(u0, u1):
+            nc.scalar.activation(
+                out=rstd[:, u0:u1], in_=sums[:, u0:u1], func=ACT.Abs_reciprocal_sqrt, scale=1.0 / E, bias=EPS
+            )
+
+        def finish(u):
+            c, h = divmod(u, H)
+            nc.vector.scalar_tensor_tensor(
+                out=o_sb[c][:, h, :],
+                in0=y_banks[c][:, h, :],
+                scalar=rstd[:, u : u + 1],
+                in1=gn_sb[:],
+                op0=ALU.mult,
+                op1=ALU.mult,
+            )
+
+        def store(c, h0, h1):
+            nc.sync.dma_start(
+                out=out[h0:h1, c * QT : (c + 1) * QT, :].rearrange("h q e -> q h e"), in_=o_sb[c][:, h0:h1, :]
+            )
+
+        load_k(0)
+        load_q(0)
+        load_k(1)
+        load_k(2)
+        nc.sync.dma_start(out=t_sb[:, 0, :], in_=t.rearrange("(p j) o -> p (j o)", j=PACK))
+        load_q(1)
+        load_v(0)
+        load_q(2)
+        load_v(1)
+        load_q(3)
+        nc.sync.dma_start(out=gn_sb[:], in_=gn[:, :])
+        nc.vector.memset(zero_in[:], 0.0)
+        nc.scalar.activation(out=zero[:], in_=zero_in[:], func=ACT.Silu)
+
+        cast_k(0)
+        cast("scalar", q_raw[0], q_bf[0], 0, QT)
+        quantize_k(0)
+        cast_k(1)
+        quantize_q(0)
+        cast_k(2)
+        quantize_k(1)
+        scores(0)
+        cast("scalar", q_raw[1], q_bf[1], 0, QT)
+        quantize_q(1)
+        scores(1)
+        cast("vector", v_raw[0], v_bf[0], 0, E)
+        cast("vector", q_raw[2], q_bf[2], 0, QT)
+        quantize_v(0)
+        silu(0)
+        silu(1)
+        weigh(0)
+        quantize_q(2)
+        scores(2)
+        weigh(1)
+        product(0)
+        cast("vector", v_raw[1], v_bf[1], 0, E)
+        cast("vector", q_raw[3], q_bf[3], 0, QT)
+        quantize_v(1)
+        silu(2)
+        silu(3)
+        product(1)
+        quantize_q(3)
+        scores(3)
+        for u in range(4, UNITS):
+            silu(u)
+        weigh(2)
+        weigh(3)
+        product(2)
+        weigh(4)
+        product(3)
+        for u in range(4):
+            square(u)
+        inverse_root(0, 4)
+        weigh(5)
+        product(4)
+        weigh(6)
+        product(5)
+        square(4)
+        square(5)
+        inverse_root(4, 6)
+        weigh(7)
+        product(6)
+        finish(0)
+        product(7)
+        finish(1)
+        store(0, 0, H)
+        square(6)
+        inverse_root(6, 7)
+        square(7)
+        inverse_root(7, 8)
+        for c in range(1, TILES - 1):
+            finish(2 * c)
+            finish(2 * c + 1)
+            store(c, 0, H)
+        for h in range(H):
+            finish(UNITS - H + h)
+            store(TILES - 1, h, h + 1)

@@ -22,7 +22,6 @@ UNITS = TILES * H
 HALF = NT // 2
 SLOTS = HALF // PACK
 EPS = 1e-5 * 16.0 * 16.0
-K_PIECES = [(0, 256), (256, 384), (384, 512)]
 
 
 def tile_rows_a_silu_onorm_kernel(tc, qT, kT, t, v, gn, out):
@@ -35,15 +34,12 @@ def tile_rows_a_silu_onorm_kernel(tc, qT, kT, t, v, gn, out):
         def tiles(name, n, shape, dtype):
             return [sb.tile(shape, dtype, name="%s%d" % (name, i), align_bytes=64) for i in range(n)]
 
-        k_raw = [
-            sb.tile([P, PACK, n1 - n0], F32, name="k_raw%d" % i, align_bytes=64)
-            for i, (n0, n1) in enumerate(K_PIECES)
-        ]
-        q_raw = tiles("q_raw", TILES, [P, PACK, QT], F32)
+        k_raw = tiles("k_raw", 2, [P, PACK, HALF], F32)
+        q_raw = tiles("q_raw", 2, [P, PACK, 2 * QT], F32)
         v_raw = tiles("v_raw", H, [P, PACK, E], F32)
         t_sb = sb.tile([P, 1, PACK], F32, name="t_sb")
         gn_sb = sb.tile([P, E], F32, name="gn_sb")
-        k_bf = tiles("k_bf", 2, [P, PACK, SLOTS, PACK], BF16)
+        k_bf = [tiles("k_bf%d_" % a, 2, [P, 2, SLOTS, PACK], BF16) for a in range(2)]
         q_bf = tiles("q_bf", TILES, [P, QT, PACK], BF16)
         v_bf = tiles("v_bf", H, [P, E, PACK], BF16)
         k_codes = tiles("k_codes", PACK, [P, P], U32)
@@ -52,10 +48,10 @@ def tile_rows_a_silu_onorm_kernel(tc, qT, kT, t, v, gn, out):
         q_scales = tiles("q_scales", TILES, [P, QT], U8)
         v_codes = tiles("v_codes", H, [P, E], U32)
         v_scales = tiles("v_scales", H, [P, E], U8)
-        p_sb = tiles("p_sb", UNITS, [P, QT, PACK], F32)
-        w_bf = tiles("w_bf", UNITS, [P, QT, PACK], BF16)
-        w_codes = tiles("w_codes", UNITS, [P, QT], U32)
-        w_scales = tiles("w_scales", UNITS, [P, QT], U8)
+        p_sb = tiles("p_sb", TILES, [P, H * QT, PACK], F32)
+        w_bf = tiles("w_bf", TILES, [P, H * QT, PACK], BF16)
+        w_codes = tiles("w_codes", TILES, [P, H * QT], U32)
+        w_scales = tiles("w_scales", TILES, [P, H * QT], U8)
         squares = tiles("squares", UNITS, [P, E], BF16)
         sums = sb.tile([P, UNITS], F32, name="sums")
         rstd = sb.tile([P, UNITS], F32, name="rstd")
@@ -65,17 +61,17 @@ def tile_rows_a_silu_onorm_kernel(tc, qT, kT, t, v, gn, out):
         score_banks = [
             [ps.tile([P, PACK, QT], F32, name="score%d_%d" % (h, i)) for i in range(2)] for h in range(H)
         ]
-        y_banks = [ps.tile([P, H, E], F32, name="y%d" % c) for c in range(TILES)]
+        y_banks = [ps.tile([P, 2, E], F32, name="y%d" % i) for i in range(4)]
+        y = [y_banks[u][:, 0, :] for u in range(4)] + [y_banks[(u + 1) % 4][:, 1, :] for u in range(4)]
 
         k_hbm = kT.rearrange("h (p j) n -> (h p) j n", j=PACK)
         q_hbm = qT.rearrange("h (p j) n -> (h p) j n", j=PACK)
 
         def load_k(a):
-            n0, n1 = K_PIECES[a]
-            nc.sync.dma_start(out=k_raw[a][:], in_=k_hbm[:, :, n0:n1])
+            nc.sync.dma_start(out=k_raw[a][:], in_=k_hbm[:, :, a * HALF : (a + 1) * HALF])
 
-        def load_q(c):
-            nc.sync.dma_start(out=q_raw[c][:], in_=q_hbm[:, :, c * QT : (c + 1) * QT])
+        def load_q(b):
+            nc.sync.dma_start(out=q_raw[b][:], in_=q_hbm[:, :, 2 * b * QT : 2 * (b + 1) * QT])
 
         def load_v(h):
             nc.sync.dma_start(out=v_raw[h][:], in_=v[h].rearrange("(p j) e -> p j e", j=PACK))
@@ -83,19 +79,23 @@ def tile_rows_a_silu_onorm_kernel(tc, qT, kT, t, v, gn, out):
         def copier(engine):
             return nc.vector.tensor_copy if engine == "vector" else nc.scalar.copy
 
-        def cast_k(a):
-            n0, n1 = K_PIECES[a]
-            half, s0 = divmod(n0 // PACK, SLOTS)
-            nc.vector.tensor_copy(
-                out=k_bf[half][:, :, s0 : s0 + (n1 - n0) // PACK, :].rearrange("p r s j -> p s j r"),
-                in_=k_raw[a][:].rearrange("p j (s r) -> p s j r", r=PACK),
+        def cast_k(engine, a, pair):
+            copier(engine)(
+                out=k_bf[a][pair][:].rearrange("p r s j -> p s j r"),
+                in_=k_raw[a][:].rearrange("p j (s r) -> p s j r", r=PACK)[:, :, :, 2 * pair : 2 * pair + 2],
             )
 
-        def cast(engine, raw, bf, c0, c1):
+        def cast(engine, raw, bf):
             copier(engine)(
-                out=bf[:, c0:c1, :].rearrange("p (g i) j -> p g j i", i=4),
-                in_=raw[:, :, c0:c1].rearrange("p j (g i) -> p g j i", i=4),
+                out=bf.rearrange("p (g i) j -> p g j i", i=4),
+                in_=raw.rearrange("p j (g i) -> p g j i", i=4),
             )
+
+        def cast_q(engine, c):
+            cast(engine, q_raw[c // 2][:, :, (c % 2) * QT : (c % 2 + 1) * QT], q_bf[c][:])
+
+        def cast_v(engine, h):
+            cast(engine, v_raw[h][:], v_bf[h][:])
 
         def quantize(codes, scales, bf):
             nc.vector.quantize_mx(out=codes.bitcast(FP8X4), scales=scales, in_=bf.rearrange("p c j -> p (c j)"))
@@ -103,7 +103,7 @@ def tile_rows_a_silu_onorm_kernel(tc, qT, kT, t, v, gn, out):
         def quantize_k(a):
             cols = slice(a * SLOTS, (a + 1) * SLOTS)
             for r in range(PACK):
-                quantize(k_codes[r][:, cols], k_scales[r][:, cols], k_bf[a][:, r, :, :])
+                quantize(k_codes[r][:, cols], k_scales[r][:, cols], k_bf[a][r // 2][:, r % 2, :, :])
 
         def quantize_q(c):
             quantize(q_codes[c][:], q_scales[c][:], q_bf[c][:])
@@ -112,8 +112,8 @@ def tile_rows_a_silu_onorm_kernel(tc, qT, kT, t, v, gn, out):
             quantize(v_codes[h][:], v_scales[h][:], v_bf[h][:])
 
         def scores(c):
-            for h in range(H):
-                for r in range(PACK):
+            for r in range(PACK):
+                for h in range(H):
                     rows = slice(ROWS * h, ROWS * (h + 1))
                     nc.tensor.matmul_mx(
                         out=score_banks[h][c % 2][:, r, :],
@@ -128,31 +128,38 @@ def tile_rows_a_silu_onorm_kernel(tc, qT, kT, t, v, gn, out):
         def silu(u):
             c, h = divmod(u, H)
             nc.scalar.activation(
-                out=p_sb[u][:], in_=score_banks[h][c % 2][:].rearrange("p r q -> p q r"), func=ACT.Silu
+                out=p_sb[c][:, h * QT : (h + 1) * QT, :],
+                in_=score_banks[h][c % 2][:].rearrange("p r q -> p q r"),
+                func=ACT.Silu,
             )
 
-        def weigh(u):
+        def weigh(c, h0, h1):
+            cols = slice(h0 * QT, h1 * QT)
             nc.vector.tensor_tensor(
-                out=w_bf[u][:], in0=p_sb[u][:], in1=t_sb[:].to_broadcast([P, QT, PACK]), op=ALU.mult
+                out=w_bf[c][:, cols, :],
+                in0=p_sb[c][:, cols, :],
+                in1=t_sb[:].to_broadcast([P, (h1 - h0) * QT, PACK]),
+                op=ALU.mult,
             )
 
-        def product(u):
-            c, h = divmod(u, H)
-            quantize(w_codes[u][:], w_scales[u][:], w_bf[u][:])
-            nc.tensor.matmul_mx(
-                out=y_banks[c][:, h, :],
-                lhsT=w_codes[u][:].bitcast(FP8X4),
-                lhsT_scale=w_scales[u][:],
-                rhs=v_codes[h][:].bitcast(FP8X4),
-                rhs_scale=v_scales[h][:],
-                start=True,
-                stop=True,
-            )
+        def product(c, h0, h1):
+            cols = slice(h0 * QT, h1 * QT)
+            quantize(w_codes[c][:, cols], w_scales[c][:, cols], w_bf[c][:, cols, :])
+            for h in range(h0, h1):
+                cols = slice(h * QT, (h + 1) * QT)
+                nc.tensor.matmul_mx(
+                    out=y[H * c + h],
+                    lhsT=w_codes[c][:, cols].bitcast(FP8X4),
+                    lhsT_scale=w_scales[c][:, cols],
+                    rhs=v_codes[h][:].bitcast(FP8X4),
+                    rhs_scale=v_scales[h][:],
+                    start=True,
+                    stop=True,
+                )
 
         def square(u):
-            c, h = divmod(u, H)
             nc.scalar.activation(
-                out=squares[u][:], in_=y_banks[c][:, h, :], func=ACT.Square, bias=zero[:], accum_out=sums[:, u : u + 1]
+                out=squares[u][:], in_=y[u], func=ACT.Square, bias=zero[:], accum_out=sums[:, u : u + 1]
             )
 
         def inverse_root(u0, u1):
@@ -164,7 +171,7 @@ def tile_rows_a_silu_onorm_kernel(tc, qT, kT, t, v, gn, out):
             c, h = divmod(u, H)
             nc.vector.scalar_tensor_tensor(
                 out=o_sb[c][:, h, :],
-                in0=y_banks[c][:, h, :],
+                in0=y[u],
                 scalar=rstd[:, u : u + 1],
                 in1=gn_sb[:],
                 op0=ALU.mult,
@@ -176,76 +183,70 @@ def tile_rows_a_silu_onorm_kernel(tc, qT, kT, t, v, gn, out):
                 out=out[h0:h1, c * QT : (c + 1) * QT, :].rearrange("h q e -> q h e"), in_=o_sb[c][:, h0:h1, :]
             )
 
+        nc.scalar.dma_start(out=t_sb[:, 0, :], in_=t.rearrange("(p j) o -> p (j o)", j=PACK))
         load_k(0)
         load_q(0)
         load_k(1)
-        load_k(2)
-        nc.sync.dma_start(out=t_sb[:, 0, :], in_=t.rearrange("(p j) o -> p (j o)", j=PACK))
         load_q(1)
         load_v(0)
-        load_q(2)
         load_v(1)
-        load_q(3)
         nc.sync.dma_start(out=gn_sb[:], in_=gn[:, :])
         nc.vector.memset(zero_in[:], 0.0)
         nc.scalar.activation(out=zero[:], in_=zero_in[:], func=ACT.Silu)
 
-        cast_k(0)
-        cast("scalar", q_raw[0], q_bf[0], 0, QT)
+        cast_k("vector", 0, 0)
+        cast_k("vector", 0, 1)
         quantize_k(0)
-        cast_k(1)
+        cast_q("vector", 0)
+        cast_q("scalar", 1)
         quantize_q(0)
-        cast_k(2)
+        quantize_q(1)
+        cast_k("vector", 1, 0)
+        cast_k("scalar", 1, 1)
         quantize_k(1)
         scores(0)
-        cast("scalar", q_raw[1], q_bf[1], 0, QT)
-        quantize_q(1)
         scores(1)
-        cast("vector", v_raw[0], v_bf[0], 0, E)
-        cast("vector", q_raw[2], q_bf[2], 0, QT)
-        quantize_v(0)
+        cast_q("vector", 2)
+        cast_q("vector", 3)
+        quantize_q(2)
+        quantize_q(3)
         silu(0)
         silu(1)
-        weigh(0)
-        quantize_q(2)
         scores(2)
-        weigh(1)
-        product(0)
-        cast("vector", v_raw[1], v_bf[1], 0, E)
-        cast("vector", q_raw[3], q_bf[3], 0, QT)
-        quantize_v(1)
         silu(2)
         silu(3)
-        product(1)
-        quantize_q(3)
         scores(3)
         for u in range(4, UNITS):
             silu(u)
-        weigh(2)
-        weigh(3)
-        product(2)
-        weigh(4)
-        product(3)
-        for u in range(4):
+        weigh(0, 0, 1)
+        cast_v("vector", 0)
+        weigh(0, 1, 2)
+        quantize_v(0)
+        product(0, 0, 1)
+        square(0)
+        inverse_root(0, 1)
+        cast_v("vector", 1)
+        weigh(1, 0, 2)
+        quantize_v(1)
+        product(0, 1, 2)
+        weigh(2, 0, 2)
+        product(1, 0, 2)
+        for u in range(1, 4):
             square(u)
-        inverse_root(0, 4)
-        weigh(5)
-        product(4)
-        weigh(6)
-        product(5)
-        square(4)
-        square(5)
-        inverse_root(4, 6)
-        weigh(7)
-        product(6)
+        inverse_root(1, 4)
+        weigh(3, 0, 1)
+        product(2, 0, 2)
+        weigh(3, 1, 2)
+        product(3, 0, 1)
         finish(0)
-        product(7)
-        finish(1)
-        store(0, 0, H)
-        square(6)
-        inverse_root(6, 7)
+        product(3, 1, 2)
+        for u in range(4, 7):
+            square(u)
+        inverse_root(4, 7)
         square(7)
         inverse_root(7, 8)
+        finish(1)
+        store(0, 0, H)
         for c in range(1, TILES - 1):
             finish(2 * c)
             finish(2 * c + 1)

@@ -19,8 +19,9 @@ ROWS = D // PACK
 QT = 128
 TILES = NQ // QT
 UNITS = TILES * H
-HALF = NT // 2
-SLOTS = HALF // PACK
+UNITS_IN_BANK = (4, 2, 1, 1)
+HALF_SET = P // 2
+RUN = 4
 EPS = 1e-5 * 16.0 * 16.0
 
 
@@ -34,20 +35,20 @@ def tile_rows_a_silu_onorm_kernel(tc, qT, kT, t, v, gn, out):
         def tiles(name, n, shape, dtype):
             return [sb.tile(shape, dtype, name="%s%d" % (name, i), align_bytes=64) for i in range(n)]
 
-        k_raw = tiles("k_raw", 2, [P, PACK, HALF], F32)
+        k_raw = sb.tile([P, PACK, NT], F32, name="k_raw")
         q_raw = tiles("q_raw", 2, [P, PACK, 2 * QT], F32)
-        v_raw = tiles("v_raw", H, [P, PACK, E], F32)
+        v_raw = sb.tile([P, H, PACK, E], F32, name="v_raw")
         t_sb = sb.tile([P, 1, PACK], F32, name="t_sb")
         gn_sb = sb.tile([P, E], F32, name="gn_sb")
-        k_bf = [tiles("k_bf%d_" % a, 2, [P, 2, SLOTS, PACK], BF16) for a in range(2)]
+        k_bf = [tiles("k_bf%d_" % half, 2, [P, 2, HALF_SET, PACK], BF16) for half in range(2)]
         q_bf = tiles("q_bf", TILES, [P, QT, PACK], BF16)
-        v_bf = tiles("v_bf", H, [P, E, PACK], BF16)
+        v_bf = sb.tile([P, H * E, PACK], BF16, name="v_bf", align_bytes=64)
         k_codes = tiles("k_codes", PACK, [P, P], U32)
         k_scales = tiles("k_scales", PACK, [P, P], U8)
         q_codes = tiles("q_codes", TILES, [P, QT], U32)
         q_scales = tiles("q_scales", TILES, [P, QT], U8)
-        v_codes = tiles("v_codes", H, [P, E], U32)
-        v_scales = tiles("v_scales", H, [P, E], U8)
+        v_codes = sb.tile([P, H * E], U32, name="v_codes", align_bytes=64)
+        v_scales = sb.tile([P, H * E], U8, name="v_scales", align_bytes=64)
         p_sb = tiles("p_sb", TILES, [P, H * QT, PACK], F32)
         w_bf = tiles("w_bf", TILES, [P, H * QT, PACK], BF16)
         w_codes = tiles("w_codes", TILES, [P, H * QT], U32)
@@ -61,55 +62,41 @@ def tile_rows_a_silu_onorm_kernel(tc, qT, kT, t, v, gn, out):
         score_banks = [
             [ps.tile([P, PACK, QT], F32, name="score%d_%d" % (h, i)) for i in range(2)] for h in range(H)
         ]
-        y_banks = [ps.tile([P, 2, E], F32, name="y%d" % i) for i in range(4)]
-        y = [y_banks[u][:, 0, :] for u in range(4)] + [y_banks[(u + 1) % 4][:, 1, :] for u in range(4)]
+        y_banks = [ps.tile([P, n, E], F32, name="y%d" % i) for i, n in enumerate(UNITS_IN_BANK)]
+        y = [bank[:, i, :] for bank, n in zip(y_banks, UNITS_IN_BANK) for i in range(n)]
 
-        k_hbm = kT.rearrange("h (p j) n -> (h p) j n", j=PACK)
-        q_hbm = qT.rearrange("h (p j) n -> (h p) j n", j=PACK)
-
-        def load_k(a):
-            nc.sync.dma_start(out=k_raw[a][:], in_=k_hbm[:, :, a * HALF : (a + 1) * HALF])
-
-        def load_q(b):
-            nc.sync.dma_start(out=q_raw[b][:], in_=q_hbm[:, :, 2 * b * QT : 2 * (b + 1) * QT])
-
-        def load_v(h):
-            nc.sync.dma_start(out=v_raw[h][:], in_=v[h].rearrange("(p j) e -> p j e", j=PACK))
-
-        def copier(engine):
-            return nc.vector.tensor_copy if engine == "vector" else nc.scalar.copy
-
-        def cast_k(engine, a, pair):
-            copier(engine)(
-                out=k_bf[a][pair][:].rearrange("p r s j -> p s j r"),
-                in_=k_raw[a][:].rearrange("p j (s r) -> p s j r", r=PACK)[:, :, :, 2 * pair : 2 * pair + 2],
+        def round_k(copy, half, pair):
+            tokens = slice(half * NT // 2, (half + 1) * NT // 2)
+            raw = k_raw[:, :, tokens].rearrange("p j (s r) -> p s j r", r=PACK)
+            copy(
+                out=k_bf[half][pair][:].rearrange("p r s j -> p s j r"),
+                in_=raw[:, :, :, 2 * pair : 2 * pair + 2],
             )
 
-        def cast(engine, raw, bf):
-            copier(engine)(
-                out=bf.rearrange("p (g i) j -> p g j i", i=4),
-                in_=raw.rearrange("p j (g i) -> p g j i", i=4),
+        def round_q(copy, c):
+            raw = q_raw[c // 2][:, :, (c % 2) * QT : (c % 2 + 1) * QT]
+            copy(
+                out=q_bf[c][:].rearrange("p (g i) j -> p g j i", i=RUN),
+                in_=raw.rearrange("p j (g i) -> p g j i", i=RUN),
             )
 
-        def cast_q(engine, c):
-            cast(engine, q_raw[c // 2][:, :, (c % 2) * QT : (c % 2 + 1) * QT], q_bf[c][:])
+        def round_v():
+            nc.vector.tensor_copy(
+                out=v_bf[:].rearrange("p (h g i) r -> p h g r i", h=H, i=RUN),
+                in_=v_raw[:].rearrange("p h r (g i) -> p h g r i", i=RUN),
+            )
 
-        def cast_v(engine, h):
-            cast(engine, v_raw[h][:], v_bf[h][:])
+        def quantize(codes, scales, values):
+            nc.vector.quantize_mx(out=codes.bitcast(FP8X4), scales=scales, in_=values.rearrange("p c j -> p (c j)"))
 
-        def quantize(codes, scales, bf):
-            nc.vector.quantize_mx(out=codes.bitcast(FP8X4), scales=scales, in_=bf.rearrange("p c j -> p (c j)"))
-
-        def quantize_k(a):
-            cols = slice(a * SLOTS, (a + 1) * SLOTS)
-            for r in range(PACK):
-                quantize(k_codes[r][:, cols], k_scales[r][:, cols], k_bf[a][r // 2][:, r % 2, :, :])
+        def quantize_k(half, pair):
+            cols = slice(half * HALF_SET, (half + 1) * HALF_SET)
+            for i in range(2):
+                r = 2 * pair + i
+                quantize(k_codes[r][:, cols], k_scales[r][:, cols], k_bf[half][pair][:, i, :, :])
 
         def quantize_q(c):
             quantize(q_codes[c][:], q_scales[c][:], q_bf[c][:])
-
-        def quantize_v(h):
-            quantize(v_codes[h][:], v_scales[h][:], v_bf[h][:])
 
         def scores(c):
             for r in range(PACK):
@@ -125,13 +112,13 @@ def tile_rows_a_silu_onorm_kernel(tc, qT, kT, t, v, gn, out):
                         stop=True,
                     )
 
-        def silu(u):
-            c, h = divmod(u, H)
-            nc.scalar.activation(
-                out=p_sb[c][:, h * QT : (h + 1) * QT, :],
-                in_=score_banks[h][c % 2][:].rearrange("p r q -> p q r"),
-                func=ACT.Silu,
-            )
+        def silu(c):
+            for h in range(H):
+                nc.scalar.activation(
+                    out=p_sb[c][:, h * QT : (h + 1) * QT, :],
+                    in_=score_banks[h][c % 2][:].rearrange("p r q -> p q r"),
+                    func=ACT.Silu,
+                )
 
         def weigh(c, h0, h1):
             cols = slice(h0 * QT, h1 * QT)
@@ -142,115 +129,115 @@ def tile_rows_a_silu_onorm_kernel(tc, qT, kT, t, v, gn, out):
                 op=ALU.mult,
             )
 
-        def product(c, h0, h1):
+        def quantize_w(c, h0, h1):
             cols = slice(h0 * QT, h1 * QT)
             quantize(w_codes[c][:, cols], w_scales[c][:, cols], w_bf[c][:, cols, :])
-            for h in range(h0, h1):
-                cols = slice(h * QT, (h + 1) * QT)
+
+        def product(c):
+            for h in range(H):
+                queries = slice(h * QT, (h + 1) * QT)
+                features = slice(h * E, (h + 1) * E)
                 nc.tensor.matmul_mx(
                     out=y[H * c + h],
-                    lhsT=w_codes[c][:, cols].bitcast(FP8X4),
-                    lhsT_scale=w_scales[c][:, cols],
-                    rhs=v_codes[h][:].bitcast(FP8X4),
-                    rhs_scale=v_scales[h][:],
+                    lhsT=w_codes[c][:, queries].bitcast(FP8X4),
+                    lhsT_scale=w_scales[c][:, queries],
+                    rhs=v_codes[:, features].bitcast(FP8X4),
+                    rhs_scale=v_scales[:, features],
                     start=True,
                     stop=True,
                 )
 
-        def square(u):
+        def sum_squares(c):
+            for h in range(H):
+                u = H * c + h
+                nc.scalar.activation(
+                    out=squares[u][:],
+                    in_=y[u],
+                    func=ACT.Square,
+                    bias=zero[:],
+                    accum_out=sums[:, u : u + 1],
+                )
+
+        def inverse_root(c):
+            units = slice(H * c, H * (c + 1))
             nc.scalar.activation(
-                out=squares[u][:], in_=y[u], func=ACT.Square, bias=zero[:], accum_out=sums[:, u : u + 1]
+                out=rstd[:, units], in_=sums[:, units], func=ACT.Abs_reciprocal_sqrt, scale=1.0 / E, bias=EPS
             )
 
-        def inverse_root(u0, u1):
-            nc.scalar.activation(
-                out=rstd[:, u0:u1], in_=sums[:, u0:u1], func=ACT.Abs_reciprocal_sqrt, scale=1.0 / E, bias=EPS
-            )
+        def finish(c):
+            for h in range(H):
+                u = H * c + h
+                nc.vector.scalar_tensor_tensor(
+                    out=o_sb[c][:, h, :],
+                    in0=y[u],
+                    scalar=rstd[:, u : u + 1],
+                    in1=gn_sb[:],
+                    op0=ALU.mult,
+                    op1=ALU.mult,
+                )
+            nc.sync.dma_start(out=out[:, c * QT : (c + 1) * QT, :].rearrange("h q e -> q h e"), in_=o_sb[c][:])
 
-        def finish(u):
-            c, h = divmod(u, H)
-            nc.vector.scalar_tensor_tensor(
-                out=o_sb[c][:, h, :],
-                in0=y[u],
-                scalar=rstd[:, u : u + 1],
-                in1=gn_sb[:],
-                op0=ALU.mult,
-                op1=ALU.mult,
-            )
-
-        def store(c, h0, h1):
-            nc.sync.dma_start(
-                out=out[h0:h1, c * QT : (c + 1) * QT, :].rearrange("h q e -> q h e"), in_=o_sb[c][:, h0:h1, :]
-            )
-
-        nc.scalar.dma_start(out=t_sb[:, 0, :], in_=t.rearrange("(p j) o -> p (j o)", j=PACK))
-        load_k(0)
-        load_q(0)
-        load_k(1)
-        load_q(1)
-        load_v(0)
-        load_v(1)
+        q_hbm = qT.rearrange("h (p j) n -> (h p) j n", j=PACK)
+        nc.sync.dma_start(out=k_raw[:], in_=kT.rearrange("h (p j) n -> (h p) j n", j=PACK))
+        for b in range(2):
+            nc.sync.dma_start(out=q_raw[b][:], in_=q_hbm[:, :, 2 * b * QT : 2 * (b + 1) * QT])
+        nc.sync.dma_start(out=v_raw[:], in_=v.rearrange("h (s r) e -> s h r e", r=PACK))
         nc.sync.dma_start(out=gn_sb[:], in_=gn[:, :])
+
         nc.vector.memset(zero_in[:], 0.0)
         nc.scalar.activation(out=zero[:], in_=zero_in[:], func=ACT.Silu)
 
-        cast_k("vector", 0, 0)
-        cast_k("vector", 0, 1)
-        quantize_k(0)
-        cast_q("vector", 0)
-        cast_q("scalar", 1)
+        round_k(nc.vector.tensor_copy, 0, 0)
+        round_k(nc.scalar.copy, 0, 1)
+        nc.scalar.dma_start(out=t_sb[:, 0, :], in_=t.rearrange("(s r) o -> s (r o)", r=PACK))
+        round_k(nc.vector.tensor_copy, 1, 0)
+        round_k(nc.scalar.copy, 1, 1)
+        quantize_k(0, 0)
+        quantize_k(1, 0)
+        quantize_k(0, 1)
+        round_q(nc.vector.tensor_copy, 0)
+        round_q(nc.scalar.copy, 1)
+        quantize_k(1, 1)
         quantize_q(0)
-        quantize_q(1)
-        cast_k("vector", 1, 0)
-        cast_k("scalar", 1, 1)
-        quantize_k(1)
         scores(0)
+        quantize_q(1)
         scores(1)
-        cast_q("vector", 2)
-        cast_q("vector", 3)
+        round_q(nc.vector.tensor_copy, 2)
+        round_q(nc.vector.tensor_copy, 3)
         quantize_q(2)
         quantize_q(3)
-        silu(0)
-        silu(1)
-        scores(2)
-        silu(2)
-        silu(3)
-        scores(3)
-        for u in range(4, UNITS):
-            silu(u)
-        weigh(0, 0, 1)
-        cast_v("vector", 0)
-        weigh(0, 1, 2)
-        quantize_v(0)
-        product(0, 0, 1)
-        square(0)
-        inverse_root(0, 1)
-        cast_v("vector", 1)
-        weigh(1, 0, 2)
-        quantize_v(1)
-        product(0, 1, 2)
-        weigh(2, 0, 2)
-        product(1, 0, 2)
-        for u in range(1, 4):
-            square(u)
-        inverse_root(1, 4)
-        weigh(3, 0, 1)
-        product(2, 0, 2)
-        weigh(3, 1, 2)
-        product(3, 0, 1)
-        finish(0)
-        product(3, 1, 2)
-        for u in range(4, 7):
-            square(u)
-        inverse_root(4, 7)
-        square(7)
-        inverse_root(7, 8)
-        finish(1)
-        store(0, 0, H)
-        for c in range(1, TILES - 1):
-            finish(2 * c)
-            finish(2 * c + 1)
-            store(c, 0, H)
+
+        for c in range(TILES):
+            silu(c)
+            if c + 2 < TILES:
+                scores(c + 2)
+
+        round_v()
+        weigh(0, 0, H)
+        quantize(v_codes[:], v_scales[:], v_bf[:])
+        quantize_w(0, 0, H)
+        product(0)
+        weigh(1, 0, H)
+        weigh(2, 0, H)
+        quantize_w(1, 0, H)
+        sum_squares(0)
+        inverse_root(0)
+        quantize_w(2, 0, H)
+        product(1)
+        product(2)
+        last = TILES - 1
         for h in range(H):
-            finish(UNITS - H + h)
-            store(TILES - 1, h, h + 1)
+            weigh(last, h, h + 1)
+        for h in range(H):
+            quantize_w(last, h, h + 1)
+        sum_squares(1)
+        sum_squares(2)
+        product(last)
+        inverse_root(1)
+        inverse_root(2)
+        finish(0)
+        finish(1)
+        sum_squares(last)
+        inverse_root(last)
+        finish(2)
+        finish(last)

@@ -19,8 +19,7 @@ ROWS = D // PACK
 QT = 128
 TILES = NQ // QT
 UNITS = TILES * H
-UNITS_IN_BANK = (4, 2, 1, 1)
-HALF_SET = P // 2
+UNITS_IN_BANK = (2, 4, 1, 1)
 RUN = 4
 EPS = 1e-5 * 16.0 * 16.0
 
@@ -40,13 +39,13 @@ def tile_rows_a_silu_onorm_kernel(tc, qT, kT, t, v, gn, out):
         v_raw = sb.tile([P, H, PACK, E], F32, name="v_raw")
         t_sb = sb.tile([P, 1, PACK], F32, name="t_sb")
         gn_sb = sb.tile([P, E], F32, name="gn_sb")
-        k_bf = [tiles("k_bf%d_" % half, 2, [P, 2, HALF_SET, PACK], BF16) for half in range(2)]
-        q_bf = tiles("q_bf", TILES, [P, QT, PACK], BF16)
+        k_bf = tiles("k_bf", 2, [P, 2, P, PACK], BF16)
+        q_bf = tiles("q_bf", 2, [P, 2 * QT, PACK], BF16)
         v_bf = sb.tile([P, H * E, PACK], BF16, name="v_bf", align_bytes=64)
         k_codes = tiles("k_codes", PACK, [P, P], U32)
         k_scales = tiles("k_scales", PACK, [P, P], U8)
-        q_codes = tiles("q_codes", TILES, [P, QT], U32)
-        q_scales = tiles("q_scales", TILES, [P, QT], U8)
+        q_codes = tiles("q_codes", 2, [P, 2 * QT], U32)
+        q_scales = tiles("q_scales", 2, [P, 2 * QT], U8)
         v_codes = sb.tile([P, H * E], U32, name="v_codes", align_bytes=64)
         v_scales = sb.tile([P, H * E], U8, name="v_scales", align_bytes=64)
         p_sb = tiles("p_sb", TILES, [P, H * QT, PACK], F32)
@@ -65,19 +64,18 @@ def tile_rows_a_silu_onorm_kernel(tc, qT, kT, t, v, gn, out):
         y_banks = [ps.tile([P, n, E], F32, name="y%d" % i) for i, n in enumerate(UNITS_IN_BANK)]
         y = [bank[:, i, :] for bank, n in zip(y_banks, UNITS_IN_BANK) for i in range(n)]
 
-        def round_k(copy, half, pair):
-            tokens = slice(half * NT // 2, (half + 1) * NT // 2)
-            raw = k_raw[:, :, tokens].rearrange("p j (s r) -> p s j r", r=PACK)
-            copy(
-                out=k_bf[half][pair][:].rearrange("p r s j -> p s j r"),
-                in_=raw[:, :, :, 2 * pair : 2 * pair + 2],
-            )
+        def round_k(copy, pair):
+            raw = k_raw[:].rearrange("p j (s r) -> p s j r", r=PACK)
+            copy(out=k_bf[pair][:].rearrange("p r s j -> p s j r"), in_=raw[:, :, :, 2 * pair : 2 * pair + 2])
 
-        def round_q(copy, c):
-            raw = q_raw[c // 2][:, :, (c % 2) * QT : (c % 2 + 1) * QT]
+        def query_columns(c, n):
+            return c // 2, slice((c % 2) * QT, (c % 2 + n) * QT)
+
+        def round_q(copy, c, n):
+            b, cols = query_columns(c, n)
             copy(
-                out=q_bf[c][:].rearrange("p (g i) j -> p g j i", i=RUN),
-                in_=raw.rearrange("p j (g i) -> p g j i", i=RUN),
+                out=q_bf[b][:, cols, :].rearrange("p (g i) j -> p g j i", i=RUN),
+                in_=q_raw[b][:, :, cols].rearrange("p j (g i) -> p g j i", i=RUN),
             )
 
         def round_v():
@@ -89,16 +87,17 @@ def tile_rows_a_silu_onorm_kernel(tc, qT, kT, t, v, gn, out):
         def quantize(codes, scales, values):
             nc.vector.quantize_mx(out=codes.bitcast(FP8X4), scales=scales, in_=values.rearrange("p c j -> p (c j)"))
 
-        def quantize_k(half, pair):
-            cols = slice(half * HALF_SET, (half + 1) * HALF_SET)
+        def quantize_k(pair):
             for i in range(2):
                 r = 2 * pair + i
-                quantize(k_codes[r][:, cols], k_scales[r][:, cols], k_bf[half][pair][:, i, :, :])
+                quantize(k_codes[r][:], k_scales[r][:], k_bf[pair][:, i, :, :])
 
-        def quantize_q(c):
-            quantize(q_codes[c][:], q_scales[c][:], q_bf[c][:])
+        def quantize_q(c, n):
+            b, cols = query_columns(c, n)
+            quantize(q_codes[b][:, cols], q_scales[b][:, cols], q_bf[b][:, cols, :])
 
         def scores(c):
+            b, cols = query_columns(c, 1)
             for r in range(PACK):
                 for h in range(H):
                     rows = slice(ROWS * h, ROWS * (h + 1))
@@ -106,8 +105,8 @@ def tile_rows_a_silu_onorm_kernel(tc, qT, kT, t, v, gn, out):
                         out=score_banks[h][c % 2][:, r, :],
                         lhsT=k_codes[r][rows, :].bitcast(FP8X4),
                         lhsT_scale=k_scales[r][rows, :],
-                        rhs=q_codes[c][rows, :].bitcast(FP8X4),
-                        rhs_scale=q_scales[c][rows, :],
+                        rhs=q_codes[b][rows, cols].bitcast(FP8X4),
+                        rhs_scale=q_scales[b][rows, cols],
                         start=True,
                         stop=True,
                     )
@@ -164,7 +163,7 @@ def tile_rows_a_silu_onorm_kernel(tc, qT, kT, t, v, gn, out):
                 out=rstd[:, units], in_=sums[:, units], func=ACT.Abs_reciprocal_sqrt, scale=1.0 / E, bias=EPS
             )
 
-        def finish(c):
+        def finish(c, queue):
             for h in range(H):
                 u = H * c + h
                 nc.vector.scalar_tensor_tensor(
@@ -175,7 +174,7 @@ def tile_rows_a_silu_onorm_kernel(tc, qT, kT, t, v, gn, out):
                     op0=ALU.mult,
                     op1=ALU.mult,
                 )
-            nc.sync.dma_start(out=out[:, c * QT : (c + 1) * QT, :].rearrange("h q e -> q h e"), in_=o_sb[c][:])
+            queue.dma_start(out=out[:, c * QT : (c + 1) * QT, :].rearrange("h q e -> q h e"), in_=o_sb[c][:])
 
         q_hbm = qT.rearrange("h (p j) n -> (h p) j n", j=PACK)
         nc.sync.dma_start(out=k_raw[:], in_=kT.rearrange("h (p j) n -> (h p) j n", j=PACK))
@@ -187,25 +186,19 @@ def tile_rows_a_silu_onorm_kernel(tc, qT, kT, t, v, gn, out):
         nc.vector.memset(zero_in[:], 0.0)
         nc.scalar.activation(out=zero[:], in_=zero_in[:], func=ACT.Silu)
 
-        round_k(nc.vector.tensor_copy, 0, 0)
-        round_k(nc.scalar.copy, 0, 1)
+        round_k(nc.vector.tensor_copy, 0)
+        round_k(nc.scalar.copy, 1)
         nc.scalar.dma_start(out=t_sb[:, 0, :], in_=t.rearrange("(s r) o -> s (r o)", r=PACK))
-        round_k(nc.vector.tensor_copy, 1, 0)
-        round_k(nc.scalar.copy, 1, 1)
-        quantize_k(0, 0)
-        quantize_k(1, 0)
-        quantize_k(0, 1)
-        round_q(nc.vector.tensor_copy, 0)
-        round_q(nc.scalar.copy, 1)
-        quantize_k(1, 1)
-        quantize_q(0)
+        quantize_k(0)
+        round_q(nc.vector.tensor_copy, 0, 1)
+        round_q(nc.scalar.copy, 1, 1)
+        quantize_k(1)
+        quantize_q(0, 1)
         scores(0)
-        quantize_q(1)
+        round_q(nc.vector.tensor_copy, 2, 2)
+        quantize_q(1, 1)
         scores(1)
-        round_q(nc.vector.tensor_copy, 2)
-        round_q(nc.vector.tensor_copy, 3)
-        quantize_q(2)
-        quantize_q(3)
+        quantize_q(2, 2)
 
         for c in range(TILES):
             silu(c)
@@ -235,9 +228,9 @@ def tile_rows_a_silu_onorm_kernel(tc, qT, kT, t, v, gn, out):
         product(last)
         inverse_root(1)
         inverse_root(2)
-        finish(0)
-        finish(1)
+        finish(0, nc.sync)
+        finish(1, nc.sync)
         sum_squares(last)
         inverse_root(last)
-        finish(2)
-        finish(last)
+        finish(2, nc.sync)
+        finish(last, nc.scalar)

from contextlib import ExitStack

import concourse.mybir as mybir

H, D, NQ, NT, E = 2, 256, 512, 512, 128
FLOPS = 2 * H * NQ * NT * (D + E)

F32 = mybir.dt.float32
BF16 = mybir.dt.bfloat16
U32 = mybir.dt.uint32
U8 = mybir.dt.uint8
FP8X4 = mybir.dt.float8_e4m3fn_x4
ACT = mybir.ActivationFunctionType
ALU = mybir.AluOpType

P = 128
PACK = 4
ROWS = D // PACK
QT = 128
TILES = NQ // QT
UNITS = TILES * H
UNITS_IN_BANK = (2, 4, 1, 1)
RUN = 4
EPS = 1e-5 * 16.0 * 16.0


def tile_rows_a_silu_onorm_kernel(tc, qT, kT, t, v, gn, out):
    nc = tc.nc
    with ExitStack() as ctx:
        sb = ctx.enter_context(tc.tile_pool(name="sb", bufs=1))
        ps = ctx.enter_context(tc.psum_pool(name="ps", bufs=1))
        ctx.enter_context(tc.manual_schedule())

        def tiles(name, n, shape, dtype):
            return [sb.tile(shape, dtype, name="%s%d" % (name, i), align_bytes=64) for i in range(n)]

        k_raw = sb.tile([P, PACK, NT], F32, name="k_raw")
        q_raw = tiles("q_raw", 2, [P, PACK, 2 * QT], F32)
        v_raw = sb.tile([P, H, PACK, E], F32, name="v_raw")
        t_sb = sb.tile([P, 1, PACK], F32, name="t_sb")
        gn_sb = sb.tile([P, E], F32, name="gn_sb")
        k_bf = tiles("k_bf", 2, [P, 2, P, PACK], BF16)
        q_bf = tiles("q_bf", 2, [P, 2 * QT, PACK], BF16)
        v_bf = sb.tile([P, H * E, PACK], BF16, name="v_bf", align_bytes=64)
        k_codes = tiles("k_codes", PACK, [P, P], U32)
        k_scales = tiles("k_scales", PACK, [P, P], U8)
        q_codes = tiles("q_codes", 2, [P, 2 * QT], U32)
        q_scales = tiles("q_scales", 2, [P, 2 * QT], U8)
        v_codes = sb.tile([P, H * E], U32, name="v_codes", align_bytes=64)
        v_scales = sb.tile([P, H * E], U8, name="v_scales", align_bytes=64)
        p_sb = tiles("p_sb", TILES, [P, H * QT, PACK], F32)
        w_bf = tiles("w_bf", TILES, [P, H * QT, PACK], BF16)
        w_codes = tiles("w_codes", TILES, [P, H * QT], U32)
        w_scales = tiles("w_scales", TILES, [P, H * QT], U8)
        squares = tiles("squares", UNITS, [P, E], BF16)
        sums = sb.tile([P, UNITS], F32, name="sums")
        rstd = sb.tile([P, UNITS], F32, name="rstd")
        zero_in = sb.tile([P, 1], F32, name="zero_in")
        zero = sb.tile([P, 1], F32, name="zero")
        o_sb = tiles("o_sb", TILES, [P, H, E], F32)
        score_banks = [
            [ps.tile([P, PACK, QT], F32, name="score%d_%d" % (h, i)) for i in range(2)] for h in range(H)
        ]
        y_banks = [ps.tile([P, n, E], F32, name="y%d" % i) for i, n in enumerate(UNITS_IN_BANK)]
        y = [bank[:, i, :] for bank, n in zip(y_banks, UNITS_IN_BANK) for i in range(n)]

        def round_k(copy, pair):
            raw = k_raw[:].rearrange("p j (s r) -> p s j r", r=PACK)
            copy(out=k_bf[pair][:].rearrange("p r s j -> p s j r"), in_=raw[:, :, :, 2 * pair : 2 * pair + 2])

        def query_columns(c, n):
            return c // 2, slice((c % 2) * QT, (c % 2 + n) * QT)

        def round_q(copy, c, n):
            b, cols = query_columns(c, n)
            copy(
                out=q_bf[b][:, cols, :].rearrange("p (g i) j -> p g j i", i=RUN),
                in_=q_raw[b][:, :, cols].rearrange("p j (g i) -> p g j i", i=RUN),
            )

        def round_v():
            nc.vector.tensor_copy(
                out=v_bf[:].rearrange("p (h g i) r -> p h g r i", h=H, i=RUN),
                in_=v_raw[:].rearrange("p h r (g i) -> p h g r i", i=RUN),
            )

        def quantize(codes, scales, values):
            nc.vector.quantize_mx(out=codes.bitcast(FP8X4), scales=scales, in_=values.rearrange("p c j -> p (c j)"))

        def quantize_k(pair):
            for i in range(2):
                r = 2 * pair + i
                quantize(k_codes[r][:], k_scales[r][:], k_bf[pair][:, i, :, :])

        def quantize_q(c, n):
            b, cols = query_columns(c, n)
            quantize(q_codes[b][:, cols], q_scales[b][:, cols], q_bf[b][:, cols, :])

        def scores(c):
            b, cols = query_columns(c, 1)
            for r in range(PACK):
                for h in range(H):
                    rows = slice(ROWS * h, ROWS * (h + 1))
                    nc.tensor.matmul_mx(
                        out=score_banks[h][c % 2][:, r, :],
                        lhsT=k_codes[r][rows, :].bitcast(FP8X4),
                        lhsT_scale=k_scales[r][rows, :],
                        rhs=q_codes[b][rows, cols].bitcast(FP8X4),
                        rhs_scale=q_scales[b][rows, cols],
                        start=True,
                        stop=True,
                    )

        def silu(c):
            for h in range(H):
                nc.scalar.activation(
                    out=p_sb[c][:, h * QT : (h + 1) * QT, :],
                    in_=score_banks[h][c % 2][:].rearrange("p r q -> p q r"),
                    func=ACT.Silu,
                )

        def weigh(c, h0, h1):
            cols = slice(h0 * QT, h1 * QT)
            nc.vector.tensor_tensor(
                out=w_bf[c][:, cols, :],
                in0=p_sb[c][:, cols, :],
                in1=t_sb[:].to_broadcast([P, (h1 - h0) * QT, PACK]),
                op=ALU.mult,
            )

        def quantize_w(c, h0, h1):
            cols = slice(h0 * QT, h1 * QT)
            quantize(w_codes[c][:, cols], w_scales[c][:, cols], w_bf[c][:, cols, :])

        def product(c):
            for h in range(H):
                queries = slice(h * QT, (h + 1) * QT)
                features = slice(h * E, (h + 1) * E)
                nc.tensor.matmul_mx(
                    out=y[H * c + h],
                    lhsT=w_codes[c][:, queries].bitcast(FP8X4),
                    lhsT_scale=w_scales[c][:, queries],
                    rhs=v_codes[:, features].bitcast(FP8X4),
                    rhs_scale=v_scales[:, features],
                    start=True,
                    stop=True,
                )

        def sum_squares(c):
            for h in range(H):
                u = H * c + h
                nc.scalar.activation(
                    out=squares[u][:],
                    in_=y[u],
                    func=ACT.Square,
                    bias=zero[:],
                    accum_out=sums[:, u : u + 1],
                )

        def inverse_root(c):
            units = slice(H * c, H * (c + 1))
            nc.scalar.activation(
                out=rstd[:, units], in_=sums[:, units], func=ACT.Abs_reciprocal_sqrt, scale=1.0 / E, bias=EPS
            )

        def finish(c, queue):
            for h in range(H):
                u = H * c + h
                nc.vector.scalar_tensor_tensor(
                    out=o_sb[c][:, h, :],
                    in0=y[u],
                    scalar=rstd[:, u : u + 1],
                    in1=gn_sb[:],
                    op0=ALU.mult,
                    op1=ALU.mult,
                )
            queue.dma_start(out=out[:, c * QT : (c + 1) * QT, :].rearrange("h q e -> q h e"), in_=o_sb[c][:])

        q_hbm = qT.rearrange("h (p j) n -> (h p) j n", j=PACK)
        nc.sync.dma_start(out=k_raw[:], in_=kT.rearrange("h (p j) n -> (h p) j n", j=PACK))
        for b in range(2):
            nc.sync.dma_start(out=q_raw[b][:], in_=q_hbm[:, :, 2 * b * QT : 2 * (b + 1) * QT])
        nc.sync.dma_start(out=v_raw[:], in_=v.rearrange("h (s r) e -> s h r e", r=PACK))
        nc.sync.dma_start(out=gn_sb[:], in_=gn[:, :])

        nc.vector.memset(zero_in[:], 0.0)
        nc.scalar.activation(out=zero[:], in_=zero_in[:], func=ACT.Silu)

        round_k(nc.vector.tensor_copy, 0)
        round_k(nc.scalar.copy, 1)
        nc.scalar.dma_start(out=t_sb[:, 0, :], in_=t.rearrange("(s r) o -> s (r o)", r=PACK))
        quantize_k(0)
        round_q(nc.vector.tensor_copy, 0, 1)
        round_q(nc.scalar.copy, 1, 1)
        quantize_k(1)
        quantize_q(0, 1)
        scores(0)
        round_q(nc.vector.tensor_copy, 2, 2)
        quantize_q(1, 1)
        scores(1)
        quantize_q(2, 2)

        for c in range(TILES):
            silu(c)
            if c + 2 < TILES:
                scores(c + 2)

        round_v()
        weigh(0, 0, H)
        quantize(v_codes[:], v_scales[:], v_bf[:])
        quantize_w(0, 0, H)
        product(0)
        weigh(1, 0, H)
        weigh(2, 0, H)
        quantize_w(1, 0, H)
        sum_squares(0)
        inverse_root(0)
        quantize_w(2, 0, H)
        product(1)
        product(2)
        last = TILES - 1
        for h in range(H):
            weigh(last, h, h + 1)
        for h in range(H):
            quantize_w(last, h, h + 1)
        sum_squares(1)
        sum_squares(2)
        product(last)
        inverse_root(1)
        inverse_root(2)
        finish(0, nc.sync)
        finish(1, nc.sync)
        sum_squares(last)
        inverse_root(last)
        finish(2, nc.sync)
        finish(last, nc.scalar)
